import numpy as np
CORES = [67,68,75,76,83,84,91,92,99,100,107,108,115,116,123,124]
N = 16
GROUPS = [[0,2,4,6,8,10,12,14],[1,3,5,7,9,11,13,15]]
def setup_inputs(rng):
    return {"x": rng.standard_normal((N, 128, 256), dtype=np.float32)}
def reference(x):
    y = np.empty((N, 128, 2048), x.dtype)
    for g in GROUPS:
        s = np.concatenate([x[r] for r in g], axis=1)
        for r in g:
            y[r] = s
    return {"y": y}

@@ -1,0 +1,79 @@
+from concourse.bass import DstId, RemoteDMATransfer
+
+W = 256
+NSLOT = 8
+OFF_CHIP = 0x00FF
+NE = 8
+
+SCRATCH = {
+    "land": ("sbuf", [128, NSLOT * W], "float32"),
+}
+SEMAPHORES = ["ld", "st", "sent"] + ["a%d" % k for k in range(NSLOT)]
+
+
+def rank_program(g, core, T, topo):
+    groups = T.tables["GROUPS"]
+    place = {}
+    relay_of = {}
+    for gi, members in enumerate(groups):
+        for k, r in enumerate(members):
+            c = T.cores[r]
+            place[c] = (gi, k)
+            mate_core = (topo.chip(c) ^ 1) * 8 + c % 8
+            if not topo.may_write(c, mate_core):
+                for h in range(topo.chip(c) * 8, topo.chip(c) * 8 + 8):
+                    if topo.die(h) == topo.die(c) and topo.may_write(h, mate_core) and h not in T.cores:
+                        relay_of[h] = c
+                        break
+    relay_for = {c: h for h, c in relay_of.items()}
+
+    def piece(k):
+        return T.land[:, k * W:(k + 1) * W]
+
+    def dst(c):
+        rid, pid, _se = topo.addr(c)
+        return DstId(rid=rid, pnc=pid)
+
+    def send(k, dests):
+        g.remote_dma_fused(
+            [RemoteDMATransfer(dst_ids=[dst(c) for c in dests], dma_engine_mask=OFF_CHIP,
+                               remote_sem=T.sem["a%d" % k], src=piece(k), dsts=[piece(k) for c in dests])],
+            local_sem=T.sem.sent)
+
+    if core in place:
+        me = core
+    elif core in relay_of:
+        me = relay_of[core]
+    else:
+        return
+    gi, k = place[me]
+    cores = [T.cores[r] for r in groups[gi]]
+    par = topo.chip(me) & 1
+    plane = [j for j in range(NSLOT) if j != k and (topo.chip(cores[j]) & 1) == par]
+    mate = [j for j in range(NSLOT) if topo.mates(topo.chip(cores[j]), topo.chip(me))][0]
+    calls = 0
+
+    if core in place:
+        g.dma_start(piece(k), T.x[:]).then_inc(T.sem.ld, 16)
+        g.wait_ge(T.sem.ld, 16)
+        if me in relay_for:
+            send(k, [relay_for[me]] + [relay_for[cores[j]] for j in plane])
+            calls += 1
+        else:
+            send(k, [cores[j] for j in plane] + [cores[mate]])
+            calls += 1
+            for j in plane:
+                g.wait_ge(T.sem["a%d" % j], NE)
+                send(j, [cores[mate]])
+                calls += 1
+        for j in range(NSLOT):
+            if j != k:
+                g.wait_ge(T.sem["a%d" % j], NE)
+        g.dma_start(T.y[:], T.land[:]).then_inc(T.sem.st, 16)
+        g.wait_ge(T.sem.st, 16)
+    else:
+        for j in [k] + plane:
+            g.wait_ge(T.sem["a%d" % j], NE)
+            send(j, [cores[mate]] if j == k else [me, cores[mate]])
+            calls += 1
+    g.wait_ge(T.sem.sent, NE * calls)

@@ -2,78 +2,91 @@ from concourse.bass import DstId, RemoteDMATransfer
 
 W = 256
 NSLOT = 8
-OFF_CHIP = 0x00FF
+LOW = 0x00FF
+HIGH = 0xFF00
 NE = 8
 
 SCRATCH = {
-    "land": ("sbuf", [128, NSLOT * W], "float32"),
+    "d": ("dram", [NSLOT, 128, W], "float32"),
 }
 SEMAPHORES = ["ld", "st", "sent"] + ["a%d" % k for k in range(NSLOT)]
 
 
+def relays_of(rank_core, all_ranks, topo):
+    ch = topo.chip(rank_core)
+    over = (ch ^ 1) * 8 + rank_core % 8
+    free = [h for h in range(ch * 8, ch * 8 + 8)
+            if topo.die(h) == topo.die(rank_core) and topo.may_write(h, over) and h not in all_ranks]
+    if topo.may_write(rank_core, over):
+        return [free[0], free[0], free[0], rank_core]
+    return [free[0], free[1], free[0], free[1]]
+
+
 def rank_program(g, core, T, topo):
-    groups = T.tables["GROUPS"]
-    place = {}
-    relay_of = {}
-    for gi, members in enumerate(groups):
-        for k, r in enumerate(members):
-            c = T.cores[r]
-            place[c] = (gi, k)
-            mate_core = (topo.chip(c) ^ 1) * 8 + c % 8
-            if not topo.may_write(c, mate_core):
-                for h in range(topo.chip(c) * 8, topo.chip(c) * 8 + 8):
-                    if topo.die(h) == topo.die(c) and topo.may_write(h, mate_core) and h not in T.cores:
-                        relay_of[h] = c
-                        break
-    relay_for = {c: h for h, c in relay_of.items()}
-
-    def piece(k):
-        return T.land[:, k * W:(k + 1) * W]
-
-    def dst(c):
-        rid, pid, _se = topo.addr(c)
-        return DstId(rid=rid, pnc=pid)
-
-    def send(k, dests):
-        g.remote_dma_fused(
-            [RemoteDMATransfer(dst_ids=[dst(c) for c in dests], dma_engine_mask=OFF_CHIP,
-                               remote_sem=T.sem["a%d" % k], src=piece(k), dsts=[piece(k) for c in dests])],
-            local_sem=T.sem.sent)
-
-    if core in place:
-        me = core
-    elif core in relay_of:
-        me = relay_of[core]
-    else:
+    ranks = list(T.cores)
+    me = None
+    for c in ranks:
+        if core == c or core in relays_of(c, ranks, topo):
+            me = c
+    if me is None:
         return
-    gi, k = place[me]
-    cores = [T.cores[r] for r in groups[gi]]
-    par = topo.chip(me) & 1
-    plane = [j for j in range(NSLOT) if j != k and (topo.chip(cores[j]) & 1) == par]
-    mate = [j for j in range(NSLOT) if topo.mates(topo.chip(cores[j]), topo.chip(me))][0]
-    calls = 0
+    members = [grp for grp in T.tables["GROUPS"] if T.rank_of(me) in grp][0]
+    cores = [ranks[r] for r in members]
+    slot = {c: k for k, c in enumerate(cores)}
+    k = slot[me]
+    chip_me = topo.chip(me)
+    ring = [c for c in cores if (topo.chip(c) & 1) == (chip_me & 1)]
+    far = [[c for c in cores if topo.mates(topo.chip(c), topo.chip(r))][0] for r in ring]
+    n = len(ring)
+    i = ring.index(me)
+    mate = far[i]
+    relay = relays_of(me, ranks, topo)
+    sent = [0]
 
-    if core in place:
-        g.dma_start(piece(k), T.x[:]).then_inc(T.sem.ld, 16)
+    def arrived(c):
+        return T.sem["a%d" % slot[c]]
+
+    def tr(owner, to, engines):
+        rid, pid, _se = topo.addr(to)
+        sent[0] += NE
+        return RemoteDMATransfer(dst_ids=[DstId(rid=rid, pnc=pid)], dma_engine_mask=engines,
+                                 remote_sem=arrived(owner), src=T.d[slot[owner]], dst=T.d[slot[owner]])
+
+    def issue(transfers):
+        g.remote_dma_fused(transfers, local_sem=T.sem.sent)
+
+    def col(c):
+        return T.y[:, slot[c] * W:(slot[c] + 1) * W]
+
+    if core == me:
+        g.sync.dma_start(col(me), T.x[:]).then_inc(T.sem.st, 16)
+        g.dma_start(T.d[k], T.x[:]).then_inc(T.sem.ld, 16)
         g.wait_ge(T.sem.ld, 16)
-        if me in relay_for:
-            send(k, [relay_for[me]] + [relay_for[cores[j]] for j in plane])
-            calls += 1
-        else:
-            send(k, [cores[j] for j in plane] + [cores[mate]])
-            calls += 1
-            for j in plane:
-                g.wait_ge(T.sem["a%d" % j], NE)
-                send(j, [cores[mate]])
-                calls += 1
-        for j in range(NSLOT):
-            if j != k:
-                g.wait_ge(T.sem["a%d" % j], NE)
-        g.dma_start(T.y[:], T.land[:]).then_inc(T.sem.st, 16)
-        g.wait_ge(T.sem.st, 16)
-    else:
-        for j in [k] + plane:
-            g.wait_ge(T.sem["a%d" % j], NE)
-            send(j, [cores[mate]] if j == k else [me, cores[mate]])
-            calls += 1
-    g.wait_ge(T.sem.sent, NE * calls)
+        for t in range(1, n):
+            nxt = ring[(i + t) % n]
+            out = [tr(me, relays_of(nxt, ranks, topo)[t], LOW)]
+            if t == 1:
+                out.append(tr(me, relay[0], HIGH))
+            issue(out)
+
+    for t in range(n):
+        if relay[t] != core:
+            continue
+        owner = ring[(i - t) % n]
+        g.wait_ge(arrived(owner), NE)
+        out = [tr(owner, mate, LOW)]
+        if t > 0 and core != me:
+            out.append(tr(owner, me, HIGH))
+        issue(out)
+
+    if core == me:
+        for t in range(1, n):
+            c = ring[(i - t) % n]
+            g.sync.wait_ge(arrived(c), NE)
+            g.sync.dma_start(col(c), T.d[slot[c]]).then_inc(T.sem.st, 16)
+        for t in range(n):
+            c = far[(i - t) % n]
+            g.scalar.wait_ge(arrived(c), NE)
+            g.scalar.dma_start(col(c), T.d[slot[c]]).then_inc(T.sem.st, 16)
+        g.wait_ge(T.sem.st, 16 * NSLOT)
+    g.wait_ge(T.sem.sent, sent[0])

from concourse.bass import DstId, RemoteDMATransfer

W = 256
NSLOT = 8
LOW = 0x00FF
HIGH = 0xFF00
NE = 8

SCRATCH = {
    "d": ("dram", [NSLOT, 128, W], "float32"),
}
SEMAPHORES = ["ld", "st", "sent"] + ["a%d" % k for k in range(NSLOT)]


def relays_of(rank_core, all_ranks, topo):
    ch = topo.chip(rank_core)
    over = (ch ^ 1) * 8 + rank_core % 8
    free = [h for h in range(ch * 8, ch * 8 + 8)
            if topo.die(h) == topo.die(rank_core) and topo.may_write(h, over) and h not in all_ranks]
    if topo.may_write(rank_core, over):
        return [free[0], free[0], free[0], rank_core]
    return [free[0], free[1], free[0], free[1]]


def rank_program(g, core, T, topo):
    ranks = list(T.cores)
    me = None
    for c in ranks:
        if core == c or core in relays_of(c, ranks, topo):
            me = c
    if me is None:
        return
    members = [grp for grp in T.tables["GROUPS"] if T.rank_of(me) in grp][0]
    cores = [ranks[r] for r in members]
    slot = {c: k for k, c in enumerate(cores)}
    k = slot[me]
    chip_me = topo.chip(me)
    ring = [c for c in cores if (topo.chip(c) & 1) == (chip_me & 1)]
    far = [[c for c in cores if topo.mates(topo.chip(c), topo.chip(r))][0] for r in ring]
    n = len(ring)
    i = ring.index(me)
    mate = far[i]
    relay = relays_of(me, ranks, topo)
    sent = [0]

    def arrived(c):
        return T.sem["a%d" % slot[c]]

    def tr(owner, to, engines):
        rid, pid, _se = topo.addr(to)
        sent[0] += NE
        return RemoteDMATransfer(dst_ids=[DstId(rid=rid, pnc=pid)], dma_engine_mask=engines,
                                 remote_sem=arrived(owner), src=T.d[slot[owner]], dst=T.d[slot[owner]])

    def issue(transfers):
        g.remote_dma_fused(transfers, local_sem=T.sem.sent)

    def col(c):
        return T.y[:, slot[c] * W:(slot[c] + 1) * W]

    if core == me:
        g.sync.dma_start(col(me), T.x[:]).then_inc(T.sem.st, 16)
        g.dma_start(T.d[k], T.x[:]).then_inc(T.sem.ld, 16)
        g.wait_ge(T.sem.ld, 16)
        for t in range(1, n):
            nxt = ring[(i + t) % n]
            out = [tr(me, relays_of(nxt, ranks, topo)[t], LOW)]
            if t == 1:
                out.append(tr(me, relay[0], HIGH))
            issue(out)

    for t in range(n):
        if relay[t] != core:
            continue
        owner = ring[(i - t) % n]
        g.wait_ge(arrived(owner), NE)
        out = [tr(owner, mate, LOW)]
        if t > 0 and core != me:
            out.append(tr(owner, me, HIGH))
        issue(out)

    if core == me:
        for t in range(1, n):
            c = ring[(i - t) % n]
            g.sync.wait_ge(arrived(c), NE)
            g.sync.dma_start(col(c), T.d[slot[c]]).then_inc(T.sem.st, 16)
        for t in range(n):
            c = far[(i - t) % n]
            g.scalar.wait_ge(arrived(c), NE)
            g.scalar.dma_start(col(c), T.d[slot[c]]).then_inc(T.sem.st, 16)
        g.wait_ge(T.sem.st, 16 * NSLOT)
    g.wait_ge(T.sem.sent, sent[0])
